import numpy as np
import ml_dtypes


def mxq(x, axis, fmt="e4m3"):
    dtype, down = {"e4m3": (ml_dtypes.float8_e4m3fn, 7), "e5m2": (ml_dtypes.float8_e5m2, 14)}[fmt]
    v = np.moveaxis(np.asarray(x, np.float32).astype(ml_dtypes.bfloat16).astype(np.float64), axis, -1)
    blocks = v.reshape(v.shape[:-1] + (-1, 32))
    amax = np.abs(blocks).max(-1, keepdims=True)
    byte = np.maximum(np.where(amax > 0, np.frexp(amax)[1] - 1 + 127, 0) - down, 1)
    scale = np.exp2(byte - 127.0)
    codes = (blocks / scale).astype(np.float32).astype(dtype).astype(np.float64)
    return np.moveaxis((codes * scale).reshape(v.shape), -1, axis)


WIDE = False


def mx_kscale(k):
    if not WIDE:
        return np.ones(k)
    levels = np.array([10, -10, 5, -5, 0])
    if k % 512:
        return np.exp2(np.random.permutation(np.resize(levels, k // 32))).repeat(32)
    a = np.empty((k // 512, 16))
    for p in range(k // 512):
        a[p, :8] = np.random.permutation(np.resize(levels, 8))
        for g in range(8):
            far = levels[np.abs(levels - a[p, g]) >= 10]
            a[p, g + 8] = far[np.random.randint(len(far))]
    return np.exp2(a.ravel()).repeat(32)


def f64(x):
    return np.asarray(x).astype(np.float64)


def striped(idx):
    return np.tile(idx.reshape(-1, 16).T, (8, 1)).astype(np.uint16)


def unstriped(offs):
    return offs[:16].T.reshape(-1).astype(np.int64)


def striped8(idx):
    return np.concatenate([x.reshape(-1, 16).T for x in idx]).astype(np.uint16)


def runs(offs, k):
    lists = np.stack([offs[16 * r : 16 * r + 16].T.reshape(-1) for r in range(8)]).astype(np.int64)
    return lists[np.arange(k) % 512 // 64]


def pack_weight(w):
    k, n = w.shape
    w = f64(np.asarray(w, np.float32).astype(ml_dtypes.bfloat16)).reshape(k // 32, 32, n)
    amax = np.abs(w).max(1)
    byte = np.clip(np.where(amax > 0, np.frexp(amax)[1] - 1 + 127 - 7, 1), 1, 254)
    scaled = (w * np.exp2(127.0 - byte)[:, None, :]).reshape(k, n).astype(np.float32)
    words = np.ascontiguousarray(scaled.reshape(k // 512, 128, 4, n).transpose(0, 1, 3, 2)).astype(ml_dtypes.float8_e4m3fn).view(np.uint8)
    return words, np.ascontiguousarray(byte.astype(np.uint8).reshape(k // 512, 16, n))


def unpack_weight(words, scales):
    g, p, n, _ = words.shape
    vals = np.ascontiguousarray(words).view(ml_dtypes.float8_e4m3fn).astype(np.float64) * np.repeat(np.exp2(scales.astype(np.float64) - 127.0), 8, axis=1)[..., None]
    return vals.transpose(0, 1, 3, 2).reshape(g * 512, n)


K, T, S, N, H, J = 512, 2048, 512, 512, 512, 512


def setup_inputs():
    n = np.random.standard_normal
    s = mx_kscale(K)[:, None]
    u = mx_kscale(S)
    packed_xT = pack_weight(n((K, T)) * s)
    return {
        "x_words": packed_xT[0],
        "x_scales": packed_xT[1],
        "wa": (n((K, H)) / np.sqrt(K) / s).astype(np.float32),
        "wb": (n((K, N)) / np.sqrt(K) / s).astype(np.float32),
        "tab": n((S, J)).astype(np.float32),
        "gt": (np.random.uniform(0.5, 1.5, (S, 1)) * u[:, None]).astype(np.float32),
        "gi": (np.random.uniform(0.5, 1.5, (S, 1)) / u[:, None]).astype(np.float32),
        "offs": striped(np.random.permutation(T)[:S]),
        "two": striped(np.random.permutation(T)[:S]),
        "n1": striped8(np.random.randint(0, J, (8, H))),
        "n2": striped8(np.random.randint(0, J, (8, H))),
        "n3": striped8(np.stack([np.random.permutation(H) for _ in range(8)])),
        "n4": striped8(np.stack([np.random.permutation(N) for _ in range(8)])),
        "n5": striped8(np.stack([np.random.permutation(N) for _ in range(8)])),
        "n6": striped8(np.stack([np.random.permutation(N) for _ in range(8)])),
        "n7": striped8(np.stack([np.random.permutation(N) for _ in range(8)])),
    }


def reference(x_words, x_scales, wa, wb, tab, gt, gi, offs, two, n1, n2, n3, n4, n5, n6, n7):
    xq = unpack_weight(x_words, x_scales)[:, unstriped(offs)]
    a = xq.T @ mxq(f64(wa), 0, "e4m3")
    z = f64(gt) * ((a[np.arange(S)[:, None], runs(n3, S)]) * (f64(tab)[np.arange(S)[:, None], runs(n1, S)]) + f64(tab)[np.arange(S)[:, None], runs(n2, S)])
    x_two = unpack_weight(x_words, x_scales)[:, unstriped(two)]
    b = x_two.T @ mxq(f64(wb), 0, "e4m3")
    z2 = f64(gi) * ((np.tanh(b[np.arange(S)[:, None], runs(n4, S)] - b)) * (b[np.arange(S)[:, None], runs(n5, S)]))
    cv = 0.0625 * ((mxq(z, 0, "e4m3").T @ mxq(z2, 0, "e4m3")))
    return 0.75 * (cv[np.arange(H)[:, None], runs(n6, H)] + cv[np.arange(H)[:, None], runs(n7, H)]) - cv

@@ -1,0 +1,216 @@
+from contextlib import ExitStack
+
+import concourse.mybir as mybir
+
+K, T, S, N, H, J = 512, 2048, 512, 512, 512, 512
+FLOPS = 2 * K * S * H + 2 * K * S * N + 2 * S * H * N
+
+F32 = mybir.dt.float32
+BF16 = mybir.dt.bfloat16
+I32 = mybir.dt.int32
+U32 = mybir.dt.uint32
+U16 = mybir.dt.uint16
+U8 = mybir.dt.uint8
+FP8X4 = mybir.dt.float8_e4m3fn_x4
+ALU = mybir.AluOpType
+ACT = mybir.ActivationFunctionType
+
+P = 128
+PACK = 4
+WINDOW = 1024
+HALF = 256
+
+
+def tile_picked_mombkindafdiflap_none_p_kernel(tc, x_words, x_scales, wa, wb, tab, gt, gi, offs, two, n1, n2, n3, n4, n5, n6, n7, out):
+    nc = tc.nc
+    with ExitStack() as ctx:
+        lists = ctx.enter_context(tc.tile_pool(name="lists", bufs=1))
+        sb = ctx.enter_context(tc.tile_pool(name="sb", bufs=1))
+        psum = ctx.enter_context(tc.psum_pool(name="psum", bufs=1))
+
+        def load_list(name, dram):
+            tile = lists.tile([P, S // 16], U16, name=name)
+            nc.sync.dma_start(tile[:], dram)
+            return tile
+
+        def tiles(name, width, dtype):
+            return [sb.tile([P, width], dtype, name="%s%d" % (name, t), align_bytes=64) for t in range(PACK)]
+
+        banks = [psum.tile([P, 512], F32, name="bank%d" % i) for i in range(8)]
+
+        xw = sb.tile([P, T], U32, name="xw", align_bytes=64)
+        xs = sb.tile([P, T], U8, name="xs", align_bytes=64)
+        tab_win = tiles("tab_win", WINDOW, F32)
+        wa_raw = sb.tile([P, PACK, H], F32, name="wa_raw", align_bytes=64)
+        wb_raw = sb.tile([P, PACK, N], F32, name="wb_raw", align_bytes=64)
+        gt_sb = sb.tile([P, PACK], F32, name="gt_sb")
+        gi_sb = sb.tile([P, PACK], F32, name="gi_sb")
+        tab_rows = tab.rearrange("(p t) c -> p t c", t=PACK)
+
+        nc.vector.memset(xs[:].bitcast(I32), 0)
+        l_n1 = load_list("l_n1", n1)
+        nc.sync.dma_start(tab_win[0][:, 0:J], tab_rows[:, 0, :])
+        nc.sync.dma_start(wa_raw[:], wa.rearrange("(p j) c -> p j c", j=PACK))
+        l_offs = load_list("l_offs", offs)
+        for q in range(4):
+            nc.scalar.dma_start(xs[32 * q : 32 * q + 4, :].bitcast(I32), x_scales[0, 4 * q : 4 * q + 4, :].bitcast(I32))
+        l_two = load_list("l_two", two)
+        nc.sync.dma_start(tab_win[1][:, 0:J], tab_rows[:, 1, :])
+        nc.sync.dma_start(xw[:].bitcast(I32), x_words[0].rearrange("p n t -> p (n t)").bitcast(I32))
+        for t in range(2, PACK):
+            nc.sync.dma_start(tab_win[t][:, 0:J], tab_rows[:, t, :])
+        l_n3 = load_list("l_n3", n3)
+        l_n2 = load_list("l_n2", n2)
+        nc.sync.dma_start(wb_raw[:], wb.rearrange("(p j) c -> p j c", j=PACK))
+        nc.sync.dma_start(gt_sb[:], gt.rearrange("(p t) o -> p (t o)", t=PACK))
+        nc.sync.dma_start(gi_sb[:], gi.rearrange("(p t) o -> p (t o)", t=PACK))
+        l_n4 = load_list("l_n4", n4)
+        l_n5 = load_list("l_n5", n5)
+        l_n6 = load_list("l_n6", n6)
+        l_n7 = load_list("l_n7", n7)
+
+        def pick_scales(name, lst):
+            picked = sb.tile([P, S], U8, name=name + "_picked", align_bytes=64)
+            nc.vector.tensor_copy(picked[:], xs[:].indirect(lst[:]))
+            return picked
+
+        def deal_scales(name, picked):
+            dealt = sb.tile([P, S], U8, name=name + "_dealt", align_bytes=64)
+            nc.vector.tensor_copy(dealt[:].rearrange("p (t m) -> p t m", t=PACK), picked[:].rearrange("p (m t) -> p t m", t=PACK))
+            return dealt
+
+        def pick_words(name, lst):
+            words = sb.tile([P, S], U32, name=name + "_words", align_bytes=64)
+            nc.vector.tensor_copy(words[:].rearrange("p (t m) -> p m t", t=PACK), xw[:].indirect(lst[:]))
+            return words
+
+        def interleave_weight(name, raw):
+            grouped = sb.tile([P, 512 * PACK], BF16, name=name + "_grouped", align_bytes=64)
+            nc.scalar.copy(
+                grouped[:].rearrange("p (c i j) -> p c j i", i=4, j=PACK),
+                raw[:].rearrange("p j (c i) -> p c j i", i=4),
+            )
+            return grouped
+
+        def quantize(name, grouped, width):
+            codes = sb.tile([P, width], U32, name=name + "_codes", align_bytes=64)
+            scales = sb.tile([P, width], U8, name=name + "_scales", align_bytes=64)
+            nc.vector.quantize_mx(out=codes[:].bitcast(FP8X4), scales=scales[:], in_=grouped[:])
+            return codes, scales
+
+        def product(acc, l_codes, l_scales, t, r_codes, r_scales):
+            cols = slice(P * t, P * (t + 1))
+            nc.tensor.matmul_mx(
+                out=acc,
+                lhsT=l_codes[:, cols].bitcast(FP8X4),
+                lhsT_scale=l_scales[:, cols],
+                rhs=r_codes[:].bitcast(FP8X4),
+                rhs_scale=r_scales[:],
+                start=True,
+                stop=True,
+            )
+
+        tab1 = tiles("tab1", H, F32)
+        nc.vector.tensor_copy(tab1[0][:], tab_win[0][:].indirect(l_n1[:]))
+        sa_picked = pick_scales("sa", l_offs)
+        sb_picked = pick_scales("sb", l_two)
+        sa = deal_scales("sa", sa_picked)
+        sbb = deal_scales("sb", sb_picked)
+        wa_g = interleave_weight("wa", wa_raw)
+        nc.vector.tensor_copy(tab1[1][:], tab_win[1][:].indirect(l_n1[:]))
+        wa_c, wa_s = quantize("wa", wa_g, H)
+        xa = pick_words("xa", l_offs)
+        xb = pick_words("xb", l_two)
+        for t in range(2, PACK):
+            nc.vector.tensor_copy(tab1[t][:], tab_win[t][:].indirect(l_n1[:]))
+
+        a_win = tiles("a_win", WINDOW, F32)
+        for t in range(PACK):
+            product(banks[t][:], xa, sa, t, wa_c, wa_s)
+            nc.scalar.copy(a_win[t][:, 0:H], banks[t][:])
+        wb_g = interleave_weight("wb", wb_raw)
+
+        prod = tiles("prod", H, F32)
+        zsum = tiles("zsum", H, F32)
+        z_bf = sb.tile([P, PACK, H], BF16, name="z_bf", align_bytes=64)
+        for t in range(PACK):
+            nc.vector.tensor_tensor(prod[t][:], a_win[t][:].indirect(l_n3[:]), tab1[t][:], ALU.mult)
+        wb_c, wb_s = quantize("wb", wb_g, N)
+        b_win = tiles("b_win", WINDOW, F32)
+        b_plain = tiles("b_plain", N, F32)
+        for t in range(PACK):
+            product(banks[4 + t][:], xb, sbb, t, wb_c, wb_s)
+            nc.scalar.copy(b_win[t][:, 0:N], banks[4 + t][:])
+            nc.scalar.copy(b_plain[t][:], banks[4 + t][:])
+        for t in range(PACK):
+            nc.vector.tensor_tensor(zsum[t][:], tab_win[t][:].indirect(l_n2[:]), prod[t][:], ALU.add)
+            nc.scalar.activation(z_bf[:, t, :], zsum[t][:], ACT.Copy, scale=gt_sb[:, t : t + 1])
+
+        diff = tiles("diff", N, F32)
+        th = tiles("th", N, F32)
+        thg = tiles("thg", N, F32)
+        for t in range(PACK):
+            nc.vector.tensor_tensor(diff[t][:], b_win[t][:].indirect(l_n4[:]), b_plain[t][:], ALU.subtract)
+            nc.scalar.activation(th[t][:], diff[t][:], ACT.Tanh)
+            nc.scalar.activation(thg[t][:], th[t][:], ACT.Copy, scale=gi_sb[:, t : t + 1])
+
+        z_g = sb.tile([P, H * PACK], BF16, name="z_g", align_bytes=64)
+        nc.scalar.copy(
+            z_g[:].rearrange("p (u m t) -> p m t u", u=4, t=PACK),
+            z_bf[:].rearrange("p t (m u) -> p m t u", u=4),
+        )
+
+        cv_win = tiles("cv_win", WINDOW, F32)
+        cv_neg = tiles("cv_neg", N, F32)
+        z2 = [sb.tile([P, PACK, HALF], F32, name="z2_%d" % h, align_bytes=64) for h in range(2)]
+        z2_g = [sb.tile([P, HALF * PACK], BF16, name="z2_g%d" % h, align_bytes=64) for h in range(2)]
+
+        def z2_half(h):
+            for t in range(PACK):
+                nc.vector.tensor_tensor(
+                    z2[h][:, t, :],
+                    b_win[t][:].indirect(l_n5[:, 16 * h : 16 * (h + 1)]),
+                    thg[t][:, HALF * h : HALF * (h + 1)],
+                    ALU.mult,
+                )
+
+        def z2_views(h):
+            return (
+                z2_g[h][:].rearrange("p (c i t) -> p c t i", i=4, t=PACK),
+                z2[h][:].rearrange("p t (c i) -> p c t i", i=4),
+            )
+
+        def cv_half(h, t, z_c, z_s, codes, scales):
+            cols = slice(HALF * h, HALF * (h + 1))
+            acc = banks[4 * h + t][:, 0:HALF]
+            product(acc, z_c, z_s, t, codes, scales)
+            nc.scalar.activation(cv_win[t][:, cols], acc, ACT.Copy, scale=0.046875)
+            nc.scalar.activation(cv_neg[t][:, cols], acc, ACT.Copy, scale=-0.0625)
+
+        z2_half(0)
+        nc.scalar.copy(*z2_views(0))
+        z_c, z_s = quantize("z", z_g, H)
+        z2_half(1)
+        c0, s0 = quantize("z2a", z2_g[0], HALF)
+        nc.vector.tensor_copy(*z2_views(1))
+        cv_half(0, 0, z_c, z_s, c0, s0)
+        c1, s1 = quantize("z2b", z2_g[1], HALF)
+        cv_half(1, 0, z_c, z_s, c1, s1)
+        for t in range(1, PACK):
+            cv_half(0, t, z_c, z_s, c0, s0)
+            cv_half(1, t, z_c, z_s, c1, s1)
+
+        part = tiles("part", N, F32)
+        res = tiles("res", N, F32)
+        out_rows = out.rearrange("(p t) c -> p t c", t=PACK)
+        for t in range(PACK):
+            nc.vector.tensor_tensor(part[t][:], cv_win[t][:].indirect(l_n6[:]), cv_neg[t][:], ALU.add)
+            if t > 0:
+                u = t - 1
+                nc.vector.tensor_tensor(res[u][:], cv_win[u][:].indirect(l_n7[:]), part[u][:], ALU.add)
+                nc.sync.dma_start(out_rows[:, u, :], res[u][:])
+        u = PACK - 1
+        for h in range(2):
+            cols = slice(HALF * h, HALF * (h + 1))
+            nc.vector.tensor_tensor(res[u][:, cols], cv_win[u][:].indirect(l_n7[:, 16 * h : 16 * (h + 1)]), part[u][:, cols], ALU.add)
+            nc.sync.dma_start(out_rows[:, u, cols], res[u][:, cols])

@@ -50,19 +50,19 @@ def tile_picked_mombkindafdiflap_none_p_kernel(tc, x_words, x_scales, wa, wb, ta
         nc.vector.memset(xs[:].bitcast(I32), 0)
         l_n1 = load_list("l_n1", n1)
         nc.sync.dma_start(tab_win[0][:, 0:J], tab_rows[:, 0, :])
-        nc.sync.dma_start(wa_raw[:], wa.rearrange("(p j) c -> p j c", j=PACK))
-        l_offs = load_list("l_offs", offs)
         for q in range(4):
-            nc.scalar.dma_start(xs[32 * q : 32 * q + 4, :].bitcast(I32), x_scales[0, 4 * q : 4 * q + 4, :].bitcast(I32))
-        l_two = load_list("l_two", two)
-        nc.sync.dma_start(tab_win[1][:, 0:J], tab_rows[:, 1, :])
-        nc.sync.dma_start(xw[:].bitcast(I32), x_words[0].rearrange("p n t -> p (n t)").bitcast(I32))
-        for t in range(2, PACK):
+            nc.sync.dma_start(xs[32 * q : 32 * q + 4, :].bitcast(I32), x_scales[0, 4 * q : 4 * q + 4, :].bitcast(I32))
+        for t in range(1, 3):
             nc.sync.dma_start(tab_win[t][:, 0:J], tab_rows[:, t, :])
+        l_offs = load_list("l_offs", offs)
+        nc.sync.dma_start(wa_raw[:], wa.rearrange("(p j) c -> p j c", j=PACK))
+        l_two = load_list("l_two", two)
+        nc.sync.dma_start(wb_raw[:], wb.rearrange("(p j) c -> p j c", j=PACK))
+        nc.sync.dma_start(tab_win[3][:, 0:J], tab_rows[:, 3, :])
+        nc.sync.dma_start(xw[:].bitcast(I32), x_words[0].rearrange("p n t -> p (n t)").bitcast(I32))
+        nc.sync.dma_start(gt_sb[:], gt.rearrange("(p t) o -> p (t o)", t=PACK))
         l_n3 = load_list("l_n3", n3)
         l_n2 = load_list("l_n2", n2)
-        nc.sync.dma_start(wb_raw[:], wb.rearrange("(p j) c -> p j c", j=PACK))
-        nc.sync.dma_start(gt_sb[:], gt.rearrange("(p t) o -> p (t o)", t=PACK))
         nc.sync.dma_start(gi_sb[:], gi.rearrange("(p t) o -> p (t o)", t=PACK))
         l_n4 = load_list("l_n4", n4)
         l_n5 = load_list("l_n5", n5)
@@ -95,7 +95,7 @@ def tile_picked_mombkindafdiflap_none_p_kernel(tc, x_words, x_scales, wa, wb, ta
         def quantize(name, grouped, width):
             codes = sb.tile([P, width], U32, name=name + "_codes", align_bytes=64)
             scales = sb.tile([P, width], U8, name=name + "_scales", align_bytes=64)
-            nc.vector.quantize_mx(out=codes[:].bitcast(FP8X4), scales=scales[:], in_=grouped[:])
+            nc.vector.quantize_mx(out=codes[:].bitcast(FP8X4), scales=scales[:], in_=grouped)
             return codes, scales
 
         def product(acc, l_codes, l_scales, t, r_codes, r_scales):
@@ -111,94 +111,111 @@ def tile_picked_mombkindafdiflap_none_p_kernel(tc, x_words, x_scales, wa, wb, ta
             )
 
         tab1 = tiles("tab1", H, F32)
-        nc.vector.tensor_copy(tab1[0][:], tab_win[0][:].indirect(l_n1[:]))
+        for t in range(3):
+            nc.vector.tensor_copy(tab1[t][:], tab_win[t][:].indirect(l_n1[:]))
         sa_picked = pick_scales("sa", l_offs)
         sb_picked = pick_scales("sb", l_two)
         sa = deal_scales("sa", sa_picked)
         sbb = deal_scales("sb", sb_picked)
         wa_g = interleave_weight("wa", wa_raw)
-        nc.vector.tensor_copy(tab1[1][:], tab_win[1][:].indirect(l_n1[:]))
-        wa_c, wa_s = quantize("wa", wa_g, H)
+        wb_g = interleave_weight("wb", wb_raw)
+        wa_c, wa_s = quantize("wa", wa_g[:], H)
+        nc.vector.tensor_copy(tab1[3][:], tab_win[3][:].indirect(l_n1[:]))
+        wb_c, wb_s = quantize("wb", wb_g[:], N)
         xa = pick_words("xa", l_offs)
         xb = pick_words("xb", l_two)
-        for t in range(2, PACK):
-            nc.vector.tensor_copy(tab1[t][:], tab_win[t][:].indirect(l_n1[:]))
 
         a_win = tiles("a_win", WINDOW, F32)
         for t in range(PACK):
             product(banks[t][:], xa, sa, t, wa_c, wa_s)
-            nc.scalar.copy(a_win[t][:, 0:H], banks[t][:])
-        wb_g = interleave_weight("wb", wb_raw)
-
-        prod = tiles("prod", H, F32)
-        zsum = tiles("zsum", H, F32)
-        z_bf = sb.tile([P, PACK, H], BF16, name="z_bf", align_bytes=64)
+            nc.scalar.activation(a_win[t][:, 0:H], banks[t][:], ACT.Copy, scale=gt_sb[:, t : t + 1])
+        gtab_win = tiles("gtab_win", WINDOW, F32)
         for t in range(PACK):
-            nc.vector.tensor_tensor(prod[t][:], a_win[t][:].indirect(l_n3[:]), tab1[t][:], ALU.mult)
-        wb_c, wb_s = quantize("wb", wb_g, N)
+            nc.scalar.activation(gtab_win[t][:, 0:J], tab_win[t][:, 0:J], ACT.Copy, scale=gt_sb[:, t : t + 1])
         b_win = tiles("b_win", WINDOW, F32)
         b_plain = tiles("b_plain", N, F32)
+        gb_win = tiles("gb_win", WINDOW, F32)
         for t in range(PACK):
             product(banks[4 + t][:], xb, sbb, t, wb_c, wb_s)
             nc.scalar.copy(b_win[t][:, 0:N], banks[4 + t][:])
             nc.scalar.copy(b_plain[t][:], banks[4 + t][:])
         for t in range(PACK):
-            nc.vector.tensor_tensor(zsum[t][:], tab_win[t][:].indirect(l_n2[:]), prod[t][:], ALU.add)
-            nc.scalar.activation(z_bf[:, t, :], zsum[t][:], ACT.Copy, scale=gt_sb[:, t : t + 1])
+            nc.scalar.activation(gb_win[t][:, 0:N], banks[4 + t][:], ACT.Copy, scale=gi_sb[:, t : t + 1])
 
-        diff = tiles("diff", N, F32)
-        th = tiles("th", N, F32)
-        thg = tiles("thg", N, F32)
+        prod = tiles("prod", H, F32)
+        z = sb.tile([P, PACK, H], F32, name="z", align_bytes=64)
         for t in range(PACK):
-            nc.vector.tensor_tensor(diff[t][:], b_win[t][:].indirect(l_n4[:]), b_plain[t][:], ALU.subtract)
-            nc.scalar.activation(th[t][:], diff[t][:], ACT.Tanh)
-            nc.scalar.activation(thg[t][:], th[t][:], ACT.Copy, scale=gi_sb[:, t : t + 1])
-
+            nc.vector.tensor_tensor(prod[t][:], a_win[t][:].indirect(l_n3[:]), tab1[t][:], ALU.mult)
+        for t in range(PACK):
+            nc.vector.tensor_tensor(z[:, t, :], gtab_win[t][:].indirect(l_n2[:]), prod[t][:], ALU.add)
         z_g = sb.tile([P, H * PACK], BF16, name="z_g", align_bytes=64)
         nc.scalar.copy(
             z_g[:].rearrange("p (u m t) -> p m t u", u=4, t=PACK),
-            z_bf[:].rearrange("p t (m u) -> p m t u", u=4),
+            z[:].rearrange("p t (m u) -> p m t u", u=4),
         )
+
+        diff = tiles("diff", N, F32)
+        th = tiles("th", N, F32)
+        for t in range(PACK):
+            nc.vector.tensor_tensor(diff[t][:], b_win[t][:].indirect(l_n4[:]), b_plain[t][:], ALU.subtract)
+            nc.scalar.activation(th[t][:], diff[t][:], ACT.Tanh)
 
         cv_win = tiles("cv_win", WINDOW, F32)
         cv_neg = tiles("cv_neg", N, F32)
-        z2 = [sb.tile([P, PACK, HALF], F32, name="z2_%d" % h, align_bytes=64) for h in range(2)]
-        z2_g = [sb.tile([P, HALF * PACK], BF16, name="z2_g%d" % h, align_bytes=64) for h in range(2)]
+        pieces = [slice(0, 256), slice(256, 384), slice(384, 512)]
+        z2_a = sb.tile([P, PACK * 256], F32, name="z2_a", align_bytes=64)
+        z2_b = sb.tile([P, PACK * 128], F32, name="z2_b", align_bytes=64)
+        z2_c = sb.tile([P, PACK * 128], F32, name="z2_c", align_bytes=64)
+        z2 = [z2_a, z2_b, z2_c]
+        g_b = sb.tile([P, PACK * 128], BF16, name="g_b", align_bytes=64)
+        g_c = sb.tile([P, PACK * 128], BF16, name="g_c", align_bytes=64)
+        z2_g = [z2_c[:].bitcast(BF16), g_b[:], g_c[:]]
 
-        def z2_half(h):
+        def z2_piece(h):
+            cols = pieces[h]
+            width = cols.stop - cols.start
             for t in range(PACK):
                 nc.vector.tensor_tensor(
-                    z2[h][:, t, :],
-                    b_win[t][:].indirect(l_n5[:, 16 * h : 16 * (h + 1)]),
-                    thg[t][:, HALF * h : HALF * (h + 1)],
+                    z2[h][:, width * t : width * (t + 1)],
+                    gb_win[t][:].indirect(l_n5[:, cols.start // 16 : cols.stop // 16]),
+                    th[t][:, cols],
                     ALU.mult,
                 )
 
         def z2_views(h):
             return (
-                z2_g[h][:].rearrange("p (c i t) -> p c t i", i=4, t=PACK),
-                z2[h][:].rearrange("p t (c i) -> p c t i", i=4),
+                z2_g[h].rearrange("p (c i t) -> p c t i", i=4, t=PACK),
+                z2[h][:].rearrange("p (t c i) -> p c t i", i=4, t=PACK),
             )
 
-        def cv_half(h, t, z_c, z_s, codes, scales):
-            cols = slice(HALF * h, HALF * (h + 1))
-            acc = banks[4 * h + t][:, 0:HALF]
-            product(acc, z_c, z_s, t, codes, scales)
+        def evacuate(t, cols, acc):
             nc.scalar.activation(cv_win[t][:, cols], acc, ACT.Copy, scale=0.046875)
             nc.scalar.activation(cv_neg[t][:, cols], acc, ACT.Copy, scale=-0.0625)
 
-        z2_half(0)
+        z2_piece(0)
         nc.scalar.copy(*z2_views(0))
-        z_c, z_s = quantize("z", z_g, H)
-        z2_half(1)
-        c0, s0 = quantize("z2a", z2_g[0], HALF)
-        nc.vector.tensor_copy(*z2_views(1))
-        cv_half(0, 0, z_c, z_s, c0, s0)
-        c1, s1 = quantize("z2b", z2_g[1], HALF)
-        cv_half(1, 0, z_c, z_s, c1, s1)
-        for t in range(1, PACK):
-            cv_half(0, t, z_c, z_s, c0, s0)
-            cv_half(1, t, z_c, z_s, c1, s1)
+        z_c, z_s = quantize("z", z_g[:], H)
+        z2_piece(1)
+        nc.scalar.copy(*z2_views(1))
+        q = [quantize("z2a", z2_g[0], 256)]
+        for t in range(2):
+            product(banks[t][:, pieces[0]], z_c, z_s, t, *q[0])
+            evacuate(t, pieces[0], banks[t][:, pieces[0]])
+        z2_piece(2)
+        q.append(quantize("z2b", z2_g[1], 128))
+        product(banks[4][:, pieces[1]], z_c, z_s, 0, *q[1])
+        evacuate(0, pieces[1], banks[4][:, pieces[1]])
+        nc.vector.tensor_copy(*z2_views(2))
+        q.append(quantize("z2c", z2_g[2], 128))
+        product(banks[5][:, pieces[2]], z_c, z_s, 0, *q[2])
+        evacuate(0, pieces[2], banks[5][:, pieces[2]])
+        for h in (1, 2):
+            product(banks[6][:, pieces[h]], z_c, z_s, 1, *q[h])
+        evacuate(1, slice(256, N), banks[6][:, 256:N])
+        for t in range(2, PACK):
+            for h in range(3):
+                product(banks[t][:, pieces[h]], z_c, z_s, t, *q[h])
+            evacuate(t, slice(0, N), banks[t][:])
 
         part = tiles("part", N, F32)
         res = tiles("res", N, F32)

@@ -26,6 +26,7 @@ def tile_picked_mombkindafdiflap_none_p_kernel(tc, x_words, x_scales, wa, wb, ta
     with ExitStack() as ctx:
         lists = ctx.enter_context(tc.tile_pool(name="lists", bufs=1))
         sb = ctx.enter_context(tc.tile_pool(name="sb", bufs=1))
+        reuse = ctx.enter_context(tc.tile_pool(name="reuse", bufs=1))
         psum = ctx.enter_context(tc.psum_pool(name="psum", bufs=1))
 
         def load_list(name, dram):
@@ -42,7 +43,7 @@ def tile_picked_mombkindafdiflap_none_p_kernel(tc, x_words, x_scales, wa, wb, ta
         xs = sb.tile([P, T], U8, name="xs", align_bytes=64)
         tab_win = tiles("tab_win", WINDOW, F32)
         wa_raw = sb.tile([P, PACK, H], F32, name="wa_raw", align_bytes=64)
-        wb_raw = sb.tile([P, PACK, N], F32, name="wb_raw", align_bytes=64)
+        wb_raw = reuse.tile([P, PACK, N], F32, name="wb_raw", offset=0)
         gt_sb = sb.tile([P, PACK], F32, name="gt_sb")
         gi_sb = sb.tile([P, PACK], F32, name="gi_sb")
         tab_rows = tab.rearrange("(p t) c -> p t c", t=PACK)
@@ -50,17 +51,17 @@ def tile_picked_mombkindafdiflap_none_p_kernel(tc, x_words, x_scales, wa, wb, ta
         nc.vector.memset(xs[:].bitcast(I32), 0)
         l_n1 = load_list("l_n1", n1)
         nc.sync.dma_start(tab_win[0][:, 0:J], tab_rows[:, 0, :])
-        for q in range(4):
-            nc.sync.dma_start(xs[32 * q : 32 * q + 4, :].bitcast(I32), x_scales[0, 4 * q : 4 * q + 4, :].bitcast(I32))
         for t in range(1, 3):
             nc.sync.dma_start(tab_win[t][:, 0:J], tab_rows[:, t, :])
-        l_offs = load_list("l_offs", offs)
         nc.sync.dma_start(wa_raw[:], wa.rearrange("(p j) c -> p j c", j=PACK))
+        l_offs = load_list("l_offs", offs)
+        for q in range(4):
+            nc.sync.dma_start(xs[32 * q : 32 * q + 4, :].bitcast(I32), x_scales[0, 4 * q : 4 * q + 4, :].bitcast(I32))
         l_two = load_list("l_two", two)
-        nc.sync.dma_start(wb_raw[:], wb.rearrange("(p j) c -> p j c", j=PACK))
-        nc.sync.dma_start(tab_win[3][:, 0:J], tab_rows[:, 3, :])
         nc.sync.dma_start(xw[:].bitcast(I32), x_words[0].rearrange("p n t -> p (n t)").bitcast(I32))
         nc.sync.dma_start(gt_sb[:], gt.rearrange("(p t) o -> p (t o)", t=PACK))
+        nc.sync.dma_start(tab_win[3][:, 0:J], tab_rows[:, 3, :])
+        nc.sync.dma_start(wb_raw[:], wb.rearrange("(p j) c -> p j c", j=PACK))
         l_n3 = load_list("l_n3", n3)
         l_n2 = load_list("l_n2", n2)
         nc.sync.dma_start(gi_sb[:], gi.rearrange("(p t) o -> p (t o)", t=PACK))
@@ -77,12 +78,12 @@ def tile_picked_mombkindafdiflap_none_p_kernel(tc, x_words, x_scales, wa, wb, ta
         def deal_scales(name, picked):
             dealt = sb.tile([P, S], U8, name=name + "_dealt", align_bytes=64)
             nc.vector.tensor_copy(dealt[:].rearrange("p (t m) -> p t m", t=PACK), picked[:].rearrange("p (m t) -> p t m", t=PACK))
-            return dealt
+            return dealt[:]
 
         def pick_words(name, lst):
             words = sb.tile([P, S], U32, name=name + "_words", align_bytes=64)
             nc.vector.tensor_copy(words[:].rearrange("p (t m) -> p m t", t=PACK), xw[:].indirect(lst[:]))
-            return words
+            return words[:]
 
         def interleave_weight(name, raw):
             grouped = sb.tile([P, 512 * PACK], BF16, name=name + "_grouped", align_bytes=64)
@@ -92,11 +93,13 @@ def tile_picked_mombkindafdiflap_none_p_kernel(tc, x_words, x_scales, wa, wb, ta
             )
             return grouped
 
-        def quantize(name, grouped, width):
+        def quantize(name, grouped, width, scales=None):
             codes = sb.tile([P, width], U32, name=name + "_codes", align_bytes=64)
-            scales = sb.tile([P, width], U8, name=name + "_scales", align_bytes=64)
-            nc.vector.quantize_mx(out=codes[:].bitcast(FP8X4), scales=scales[:], in_=grouped)
-            return codes, scales
+            if scales is None:
+                plane = sb.tile([P, width], U8, name=name + "_scales", align_bytes=64)
+                scales = plane[:]
+            nc.vector.quantize_mx(out=codes[:].bitcast(FP8X4), scales=scales, in_=grouped)
+            return codes[:], scales
 
         def product(acc, l_codes, l_scales, t, r_codes, r_scales):
             cols = slice(P * t, P * (t + 1))
@@ -104,8 +107,8 @@ def tile_picked_mombkindafdiflap_none_p_kernel(tc, x_words, x_scales, wa, wb, ta
                 out=acc,
                 lhsT=l_codes[:, cols].bitcast(FP8X4),
                 lhsT_scale=l_scales[:, cols],
-                rhs=r_codes[:].bitcast(FP8X4),
-                rhs_scale=r_scales[:],
+                rhs=r_codes.bitcast(FP8X4),
+                rhs_scale=r_scales,
                 start=True,
                 stop=True,
             )
@@ -120,18 +123,18 @@ def tile_picked_mombkindafdiflap_none_p_kernel(tc, x_words, x_scales, wa, wb, ta
         wa_g = interleave_weight("wa", wa_raw)
         wb_g = interleave_weight("wb", wb_raw)
         wa_c, wa_s = quantize("wa", wa_g[:], H)
-        nc.vector.tensor_copy(tab1[3][:], tab_win[3][:].indirect(l_n1[:]))
-        wb_c, wb_s = quantize("wb", wb_g[:], N)
         xa = pick_words("xa", l_offs)
         xb = pick_words("xb", l_two)
+        nc.vector.tensor_copy(tab1[3][:], tab_win[3][:].indirect(l_n1[:]))
+        wb_c, wb_s = quantize("wb", wb_g[:], N)
 
-        a_win = tiles("a_win", WINDOW, F32)
-        for t in range(PACK):
-            product(banks[t][:], xa, sa, t, wa_c, wa_s)
-            nc.scalar.activation(a_win[t][:, 0:H], banks[t][:], ACT.Copy, scale=gt_sb[:, t : t + 1])
         gtab_win = tiles("gtab_win", WINDOW, F32)
         for t in range(PACK):
             nc.scalar.activation(gtab_win[t][:, 0:J], tab_win[t][:, 0:J], ACT.Copy, scale=gt_sb[:, t : t + 1])
+        a_win = [reuse.tile([P, WINDOW], F32, name="a_win%d" % t, offset=4 * WINDOW * t) for t in range(PACK)]
+        for t in range(PACK):
+            product(banks[t % 2][:], xa, sa, t, wa_c, wa_s)
+            nc.scalar.activation(a_win[t][:, 0:H], banks[t % 2][:], ACT.Copy, scale=gt_sb[:, t : t + 1])
         b_win = tiles("b_win", WINDOW, F32)
         b_plain = tiles("b_plain", N, F32)
         gb_win = tiles("gb_win", WINDOW, F32)
@@ -164,12 +167,12 @@ def tile_picked_mombkindafdiflap_none_p_kernel(tc, x_words, x_scales, wa, wb, ta
         cv_neg = tiles("cv_neg", N, F32)
         pieces = [slice(0, 256), slice(256, 384), slice(384, 512)]
         z2_a = sb.tile([P, PACK * 256], F32, name="z2_a", align_bytes=64)
-        z2_b = sb.tile([P, PACK * 128], F32, name="z2_b", align_bytes=64)
-        z2_c = sb.tile([P, PACK * 128], F32, name="z2_c", align_bytes=64)
-        z2 = [z2_a, z2_b, z2_c]
+        z2_b = diff[PACK - 1]
+        z2 = [z2_a[:], z2_b[:], z2_a[:, 0 : PACK * 128]]
+        g_a = sb.tile([P, PACK * 256], BF16, name="g_a", align_bytes=64)
         g_b = sb.tile([P, PACK * 128], BF16, name="g_b", align_bytes=64)
         g_c = sb.tile([P, PACK * 128], BF16, name="g_c", align_bytes=64)
-        z2_g = [z2_c[:].bitcast(BF16), g_b[:], g_c[:]]
+        z2_g = [g_a[:], g_b[:], g_c[:]]
 
         def z2_piece(h):
             cols = pieces[h]
@@ -185,7 +188,7 @@ def tile_picked_mombkindafdiflap_none_p_kernel(tc, x_words, x_scales, wa, wb, ta
         def z2_views(h):
             return (
                 z2_g[h].rearrange("p (c i t) -> p c t i", i=4, t=PACK),
-                z2[h][:].rearrange("p (t c i) -> p c t i", i=4, t=PACK),
+                z2[h].rearrange("p (t c i) -> p c t i", i=4, t=PACK),
             )
 
         def evacuate(t, cols, acc):
@@ -194,7 +197,7 @@ def tile_picked_mombkindafdiflap_none_p_kernel(tc, x_words, x_scales, wa, wb, ta
 
         z2_piece(0)
         nc.scalar.copy(*z2_views(0))
-        z_c, z_s = quantize("z", z_g[:], H)
+        z_c, z_s = quantize("z01", z_g[:, 0:1024], 256)
         z2_piece(1)
         nc.scalar.copy(*z2_views(1))
         q = [quantize("z2a", z2_g[0], 256)]
@@ -206,22 +209,29 @@ def tile_picked_mombkindafdiflap_none_p_kernel(tc, x_words, x_scales, wa, wb, ta
         product(banks[4][:, pieces[1]], z_c, z_s, 0, *q[1])
         evacuate(0, pieces[1], banks[4][:, pieces[1]])
         nc.vector.tensor_copy(*z2_views(2))
-        q.append(quantize("z2c", z2_g[2], 128))
+        late = sb.tile([P, 256], U8, name="late_planes", align_bytes=64)
+        q.append(quantize("z2c", z2_g[2], 128, late[:, 0:128]))
         product(banks[5][:, pieces[2]], z_c, z_s, 0, *q[2])
         evacuate(0, pieces[2], banks[5][:, pieces[2]])
         for h in (1, 2):
             product(banks[6][:, pieces[h]], z_c, z_s, 1, *q[h])
         evacuate(1, slice(256, N), banks[6][:, 256:N])
+        z_c, z_s = quantize("z23", z_g[:, 1024:2048], 256, late[4:P, :])
         for t in range(2, PACK):
             for h in range(3):
-                product(banks[t][:, pieces[h]], z_c, z_s, t, *q[h])
+                product(banks[t][:, pieces[h]], z_c, z_s, t - 2, *q[h])
             evacuate(t, slice(0, N), banks[t][:])
 
         part = tiles("part", N, F32)
         res = tiles("res", N, F32)
         out_rows = out.rearrange("(p t) c -> p t c", t=PACK)
         for t in range(PACK):
-            nc.vector.tensor_tensor(part[t][:], cv_win[t][:].indirect(l_n6[:]), cv_neg[t][:], ALU.add)
+            if t == 0:
+                for h in range(2):
+                    cols = slice(HALF * h, HALF * (h + 1))
+                    nc.vector.tensor_tensor(part[t][:, cols], cv_win[t][:].indirect(l_n6[:, 16 * h : 16 * (h + 1)]), cv_neg[t][:, cols], ALU.add)
+            else:
+                nc.vector.tensor_tensor(part[t][:], cv_win[t][:].indirect(l_n6[:]), cv_neg[t][:], ALU.add)
             if t > 0:
                 u = t - 1
                 nc.vector.tensor_tensor(res[u][:], cv_win[u][:].indirect(l_n7[:]), part[u][:], ALU.add)

from contextlib import ExitStack

import concourse.mybir as mybir

K, T, S, N, H, J = 512, 2048, 512, 512, 512, 512
FLOPS = 2 * K * S * H + 2 * K * S * N + 2 * S * H * N

F32 = mybir.dt.float32
BF16 = mybir.dt.bfloat16
I32 = mybir.dt.int32
U32 = mybir.dt.uint32
U16 = mybir.dt.uint16
U8 = mybir.dt.uint8
FP8X4 = mybir.dt.float8_e4m3fn_x4
ALU = mybir.AluOpType
ACT = mybir.ActivationFunctionType

P = 128
PACK = 4
WINDOW = 1024
HALF = 256


def tile_picked_mombkindafdiflap_none_p_kernel(tc, x_words, x_scales, wa, wb, tab, gt, gi, offs, two, n1, n2, n3, n4, n5, n6, n7, out):
    nc = tc.nc
    with ExitStack() as ctx:
        lists = ctx.enter_context(tc.tile_pool(name="lists", bufs=1))
        sb = ctx.enter_context(tc.tile_pool(name="sb", bufs=1))
        reuse = ctx.enter_context(tc.tile_pool(name="reuse", bufs=1))
        psum = ctx.enter_context(tc.psum_pool(name="psum", bufs=1))

        def load_list(name, dram):
            tile = lists.tile([P, S // 16], U16, name=name)
            nc.sync.dma_start(tile[:], dram)
            return tile

        def tiles(name, width, dtype):
            return [sb.tile([P, width], dtype, name="%s%d" % (name, t), align_bytes=64) for t in range(PACK)]

        banks = [psum.tile([P, 512], F32, name="bank%d" % i) for i in range(8)]

        xw = sb.tile([P, T], U32, name="xw", align_bytes=64)
        xs = sb.tile([P, T], U8, name="xs", align_bytes=64)
        tab_win = tiles("tab_win", WINDOW, F32)
        wa_raw = sb.tile([P, PACK, H], F32, name="wa_raw", align_bytes=64)
        wb_raw = reuse.tile([P, PACK, N], F32, name="wb_raw", offset=0)
        gt_sb = sb.tile([P, PACK], F32, name="gt_sb")
        gi_sb = sb.tile([P, PACK], F32, name="gi_sb")
        tab_rows = tab.rearrange("(p t) c -> p t c", t=PACK)

        nc.vector.memset(xs[:].bitcast(I32), 0)
        l_n1 = load_list("l_n1", n1)
        nc.sync.dma_start(tab_win[0][:, 0:J], tab_rows[:, 0, :])
        for t in range(1, 3):
            nc.sync.dma_start(tab_win[t][:, 0:J], tab_rows[:, t, :])
        nc.sync.dma_start(wa_raw[:], wa.rearrange("(p j) c -> p j c", j=PACK))
        l_offs = load_list("l_offs", offs)
        for q in range(4):
            nc.sync.dma_start(xs[32 * q : 32 * q + 4, :].bitcast(I32), x_scales[0, 4 * q : 4 * q + 4, :].bitcast(I32))
        l_two = load_list("l_two", two)
        nc.sync.dma_start(xw[:].bitcast(I32), x_words[0].rearrange("p n t -> p (n t)").bitcast(I32))
        nc.sync.dma_start(gt_sb[:], gt.rearrange("(p t) o -> p (t o)", t=PACK))
        nc.sync.dma_start(tab_win[3][:, 0:J], tab_rows[:, 3, :])
        nc.sync.dma_start(wb_raw[:], wb.rearrange("(p j) c -> p j c", j=PACK))
        l_n3 = load_list("l_n3", n3)
        l_n2 = load_list("l_n2", n2)
        nc.sync.dma_start(gi_sb[:], gi.rearrange("(p t) o -> p (t o)", t=PACK))
        l_n4 = load_list("l_n4", n4)
        l_n5 = load_list("l_n5", n5)
        l_n6 = load_list("l_n6", n6)
        l_n7 = load_list("l_n7", n7)

        def pick_scales(name, lst):
            picked = sb.tile([P, S], U8, name=name + "_picked", align_bytes=64)
            nc.vector.tensor_copy(picked[:], xs[:].indirect(lst[:]))
            return picked

        def deal_scales(name, picked):
            dealt = sb.tile([P, S], U8, name=name + "_dealt", align_bytes=64)
            nc.vector.tensor_copy(dealt[:].rearrange("p (t m) -> p t m", t=PACK), picked[:].rearrange("p (m t) -> p t m", t=PACK))
            return dealt[:]

        def pick_words(name, lst):
            words = sb.tile([P, S], U32, name=name + "_words", align_bytes=64)
            nc.vector.tensor_copy(words[:].rearrange("p (t m) -> p m t", t=PACK), xw[:].indirect(lst[:]))
            return words[:]

        def interleave_weight(name, raw):
            grouped = sb.tile([P, 512 * PACK], BF16, name=name + "_grouped", align_bytes=64)
            nc.scalar.copy(
                grouped[:].rearrange("p (c i j) -> p c j i", i=4, j=PACK),
                raw[:].rearrange("p j (c i) -> p c j i", i=4),
            )
            return grouped

        def quantize(name, grouped, width, scales=None):
            codes = sb.tile([P, width], U32, name=name + "_codes", align_bytes=64)
            if scales is None:
                plane = sb.tile([P, width], U8, name=name + "_scales", align_bytes=64)
                scales = plane[:]
            nc.vector.quantize_mx(out=codes[:].bitcast(FP8X4), scales=scales, in_=grouped)
            return codes[:], scales

        def product(acc, l_codes, l_scales, t, r_codes, r_scales):
            cols = slice(P * t, P * (t + 1))
            nc.tensor.matmul_mx(
                out=acc,
                lhsT=l_codes[:, cols].bitcast(FP8X4),
                lhsT_scale=l_scales[:, cols],
                rhs=r_codes.bitcast(FP8X4),
                rhs_scale=r_scales,
                start=True,
                stop=True,
            )

        tab1 = tiles("tab1", H, F32)
        for t in range(3):
            nc.vector.tensor_copy(tab1[t][:], tab_win[t][:].indirect(l_n1[:]))
        sa_picked = pick_scales("sa", l_offs)
        sb_picked = pick_scales("sb", l_two)
        sa = deal_scales("sa", sa_picked)
        sbb = deal_scales("sb", sb_picked)
        wa_g = interleave_weight("wa", wa_raw)
        wb_g = interleave_weight("wb", wb_raw)
        wa_c, wa_s = quantize("wa", wa_g[:], H)
        xa = pick_words("xa", l_offs)
        xb = pick_words("xb", l_two)
        nc.vector.tensor_copy(tab1[3][:], tab_win[3][:].indirect(l_n1[:]))
        wb_c, wb_s = quantize("wb", wb_g[:], N)

        gtab_win = tiles("gtab_win", WINDOW, F32)
        for t in range(PACK):
            nc.scalar.activation(gtab_win[t][:, 0:J], tab_win[t][:, 0:J], ACT.Copy, scale=gt_sb[:, t : t + 1])
        a_win = [reuse.tile([P, WINDOW], F32, name="a_win%d" % t, offset=4 * WINDOW * t) for t in range(PACK)]
        for t in range(PACK):
            product(banks[t % 2][:], xa, sa, t, wa_c, wa_s)
            nc.scalar.activation(a_win[t][:, 0:H], banks[t % 2][:], ACT.Copy, scale=gt_sb[:, t : t + 1])
        b_win = tiles("b_win", WINDOW, F32)
        b_plain = tiles("b_plain", N, F32)
        gb_win = tiles("gb_win", WINDOW, F32)
        for t in range(PACK):
            product(banks[4 + t][:], xb, sbb, t, wb_c, wb_s)
            nc.scalar.copy(b_win[t][:, 0:N], banks[4 + t][:])
            nc.scalar.copy(b_plain[t][:], banks[4 + t][:])
        for t in range(PACK):
            nc.scalar.activation(gb_win[t][:, 0:N], banks[4 + t][:], ACT.Copy, scale=gi_sb[:, t : t + 1])

        prod = tiles("prod", H, F32)
        z = sb.tile([P, PACK, H], F32, name="z", align_bytes=64)
        for t in range(PACK):
            nc.vector.tensor_tensor(prod[t][:], a_win[t][:].indirect(l_n3[:]), tab1[t][:], ALU.mult)
        for t in range(PACK):
            nc.vector.tensor_tensor(z[:, t, :], gtab_win[t][:].indirect(l_n2[:]), prod[t][:], ALU.add)
        z_g = sb.tile([P, H * PACK], BF16, name="z_g", align_bytes=64)
        nc.scalar.copy(
            z_g[:].rearrange("p (u m t) -> p m t u", u=4, t=PACK),
            z[:].rearrange("p t (m u) -> p m t u", u=4),
        )

        diff = tiles("diff", N, F32)
        th = tiles("th", N, F32)
        for t in range(PACK):
            nc.vector.tensor_tensor(diff[t][:], b_win[t][:].indirect(l_n4[:]), b_plain[t][:], ALU.subtract)
            nc.scalar.activation(th[t][:], diff[t][:], ACT.Tanh)

        cv_win = tiles("cv_win", WINDOW, F32)
        cv_neg = tiles("cv_neg", N, F32)
        pieces = [slice(0, 256), slice(256, 384), slice(384, 512)]
        z2_a = sb.tile([P, PACK * 256], F32, name="z2_a", align_bytes=64)
        z2_b = diff[PACK - 1]
        z2 = [z2_a[:], z2_b[:], z2_a[:, 0 : PACK * 128]]
        g_a = sb.tile([P, PACK * 256], BF16, name="g_a", align_bytes=64)
        g_b = sb.tile([P, PACK * 128], BF16, name="g_b", align_bytes=64)
        g_c = sb.tile([P, PACK * 128], BF16, name="g_c", align_bytes=64)
        z2_g = [g_a[:], g_b[:], g_c[:]]

        def z2_piece(h):
            cols = pieces[h]
            width = cols.stop - cols.start
            for t in range(PACK):
                nc.vector.tensor_tensor(
                    z2[h][:, width * t : width * (t + 1)],
                    gb_win[t][:].indirect(l_n5[:, cols.start // 16 : cols.stop // 16]),
                    th[t][:, cols],
                    ALU.mult,
                )

        def z2_views(h):
            return (
                z2_g[h].rearrange("p (c i t) -> p c t i", i=4, t=PACK),
                z2[h].rearrange("p (t c i) -> p c t i", i=4, t=PACK),
            )

        def evacuate(t, cols, acc):
            nc.scalar.activation(cv_win[t][:, cols], acc, ACT.Copy, scale=0.046875)
            nc.scalar.activation(cv_neg[t][:, cols], acc, ACT.Copy, scale=-0.0625)

        z2_piece(0)
        nc.scalar.copy(*z2_views(0))
        z_c, z_s = quantize("z01", z_g[:, 0:1024], 256)
        z2_piece(1)
        nc.scalar.copy(*z2_views(1))
        q = [quantize("z2a", z2_g[0], 256)]
        for t in range(2):
            product(banks[t][:, pieces[0]], z_c, z_s, t, *q[0])
            evacuate(t, pieces[0], banks[t][:, pieces[0]])
        z2_piece(2)
        q.append(quantize("z2b", z2_g[1], 128))
        product(banks[4][:, pieces[1]], z_c, z_s, 0, *q[1])
        evacuate(0, pieces[1], banks[4][:, pieces[1]])
        nc.vector.tensor_copy(*z2_views(2))
        late = sb.tile([P, 256], U8, name="late_planes", align_bytes=64)
        q.append(quantize("z2c", z2_g[2], 128, late[:, 0:128]))
        product(banks[5][:, pieces[2]], z_c, z_s, 0, *q[2])
        evacuate(0, pieces[2], banks[5][:, pieces[2]])
        for h in (1, 2):
            product(banks[6][:, pieces[h]], z_c, z_s, 1, *q[h])
        evacuate(1, slice(256, N), banks[6][:, 256:N])
        z_c, z_s = quantize("z23", z_g[:, 1024:2048], 256, late[4:P, :])
        for t in range(2, PACK):
            for h in range(3):
                product(banks[t][:, pieces[h]], z_c, z_s, t - 2, *q[h])
            evacuate(t, slice(0, N), banks[t][:])

        part = tiles("part", N, F32)
        res = tiles("res", N, F32)
        out_rows = out.rearrange("(p t) c -> p t c", t=PACK)
        for t in range(PACK):
            if t == 0:
                for h in range(2):
                    cols = slice(HALF * h, HALF * (h + 1))
                    nc.vector.tensor_tensor(part[t][:, cols], cv_win[t][:].indirect(l_n6[:, 16 * h : 16 * (h + 1)]), cv_neg[t][:, cols], ALU.add)
            else:
                nc.vector.tensor_tensor(part[t][:], cv_win[t][:].indirect(l_n6[:]), cv_neg[t][:], ALU.add)
            if t > 0:
                u = t - 1
                nc.vector.tensor_tensor(res[u][:], cv_win[u][:].indirect(l_n7[:]), part[u][:], ALU.add)
                nc.sync.dma_start(out_rows[:, u, :], res[u][:])
        u = PACK - 1
        for h in range(2):
            cols = slice(HALF * h, HALF * (h + 1))
            nc.vector.tensor_tensor(res[u][:, cols], cv_win[u][:].indirect(l_n7[:, 16 * h : 16 * (h + 1)]), part[u][:, cols], ALU.add)
            nc.sync.dma_start(out_rows[:, u, cols], res[u][:, cols])
